import numpy as np, ml_dtypes
CORES = [16,32,48,64,80]
N = 5
KT, C = 1, 128
def setup_inputs(rng):
    return {"x": rng.standard_normal((N, 128, KT * C), dtype=np.float32).astype(ml_dtypes.bfloat16)}
def setup_inputs_big(rng):
    d = setup_inputs(rng)
    for k in ("x",): d[k] = (d[k].astype(np.float32) * 1024.0).astype(d[k].dtype)
    return d
def setup_inputs_small(rng):
    d = setup_inputs(rng)
    for k in ("x",): d[k] = (d[k].astype(np.float32) * (1 / 1024.0)).astype(d[k].dtype)
    return d
def setup_inputs_apart(rng):
    d = setup_inputs(rng)
    f = (10.0 ** rng.permutation(np.linspace(-1.5, 1.5, N))).astype(np.float32).reshape(N, 1, 1)
    for k in ("x",): d[k] = (d[k].astype(np.float32) * f).astype(d[k].dtype)
    return d
def reference(x):
    X = x.astype(np.float64)
    y = np.full((N, C, N * C), np.nan)
    for r in range(N):
        for i in range(N):
            s = i
            if s != r: y[r][:, C * i:C * i + C] = sum(X[r][:, C * t:C * t + C].T @ X[s][:, C * t:C * t + C] for t in range(KT))
    return {"y": y.astype(ml_dtypes.bfloat16 if x.dtype != np.float64 else np.float64)}

from concourse.bass import DstId, RemoteDMATransfer

N = 5
C = 128

SCRATCH = {}
for _s in range(N):
    SCRATCH["xs%d" % _s] = ("sbuf", [128, C], "bfloat16")
for _k in range(1, N):
    SCRATCH["ps%d" % _k] = ("psum", [128, 512], "float32")
    SCRATCH["ob%d" % _k] = ("sbuf", [128, C], "bfloat16")

SEMAPHORES = (["loaded", "sent", "stored"] + ["arr%d" % s for s in range(N)]
              + ["mm%d" % k for k in range(1, N)] + ["cp%d" % k for k in range(1, N)])


def rank_program(g, core, T, topo):
    r = T.rank_of(core)
    if r is None:
        return
    n = len(T.cores)
    own = T["xs%d" % r]

    g.sync.dma_start(own[:], T.x[:]).then_inc(T.sem.loaded, 16)

    peers = [T.cores[(r + k) % n] for k in range(1, n)]
    mask = topo.mask(core, peers[0])
    for d in peers:
        assert topo.may_write(core, d)
        mask &= topo.mask(core, d)
    engines = bin(mask).count("1")
    g.wait_ge(T.sem.loaded, 16)
    g.remote_dma_fused(
        [RemoteDMATransfer(dst_ids=[DstId(rid=topo.addr(d)[0], pnc=topo.addr(d)[1]) for d in peers],
                           dma_engine_mask=mask, remote_sem=T.sem["arr%d" % r],
                           srcs=[own[:]], dsts=[own[:] for d in peers], alu_op=0)],
        local_sem=T.sem.sent)

    g.tensor.wait_ge(T.sem.loaded, 16)
    for k in range(1, n):
        s = (r - k) % n
        ps, ob = T["ps%d" % k], T["ob%d" % k]
        g.tensor.wait_ge(T.sem["arr%d" % s], engines)
        g.tensor.matmul(ps[:, 0:C], own[:], T["xs%d" % s][:], start=True, stop=True).then_inc(T.sem["mm%d" % k], 1)
        g.vector.wait_ge(T.sem["mm%d" % k], 1)
        g.vector.tensor_copy(ob[:], ps[:, 0:C]).then_inc(T.sem["cp%d" % k], 1)
        q = g.scalar if k % 2 else g.sync
        q.wait_ge(T.sem["cp%d" % k], 1)
        q.dma_start(T.y[:, s * C:(s + 1) * C], ob[:]).then_inc(T.sem.stored, 16)

    g.wait_ge(T.sem.sent, engines)
    g.wait_ge(T.sem.stored, 16 * (n - 1))
